import numpy as np
CORES = [38,166,294,422]
N = 4
def setup_inputs(rng):
    return {"x1": rng.standard_normal((N, 128, 4), dtype=np.float32), "x2": rng.standard_normal((N, 128, 896), dtype=np.float32)}
def reference(x1, x2):
    out = []
    b = 4 // N
    bl = x1.reshape(N, 128, N, b)
    out.append(np.ascontiguousarray(bl.transpose(2, 1, 0, 3)).reshape(N, 128, 4))
    s = x2.sum(axis=0, dtype=np.float64).astype(x2.dtype)
    out.append(np.broadcast_to(s, (N,) + s.shape))
    return {"y1": out[0], "y2": out[1]}

@@ -1,0 +1,141 @@
+import concourse.bass as bass
+from concourse.mybir import AluOpType
+
+W = 896
+CHIP, RK = 4, 6
+LANES = ((0, 0, 128, "A"), (1, 128, 256, "B"), (2, 256, 384, "A"), (3, 384, 512, "B"),
+         (4, 512, 640, "A"), (5, 640, 768, "B"), (7, 768, 896, "A"))
+
+SCRATCH = {
+    "A": ("sbuf", [128, W], "float32"),
+    "R1": ("sbuf", [128, W], "float32"),
+    "P": ("sbuf", [128, W], "float32"),
+    "R2": ("sbuf", [128, W], "float32"),
+    "X1": ("sbuf", [128, 4], "float32"),
+    "Y1B": ("sbuf", [128, 4], "float32"),
+    "FW": ("sbuf", [128, 1], "float32"),
+}
+SEMAPHORES = ["ld_h", "ld_o", "ld_x", "l_c", "cp_o", "ac_o", "cp_h", "fin", "st1",
+              "own_arr", "r1_0", "r1_1", "p_arr", "r2_arr", "fw_arr", "y1_arr", "sent"]
+
+
+def nbr(h, side):
+    return h ^ 1 if side == "A" else 3 - h
+
+
+def other(side):
+    return "B" if side == "A" else "A"
+
+
+def at(h, k):
+    return h * 128 + CHIP * 8 + k
+
+
+def rank_program(g, core, T, topo):
+    if topo.chip(core) != CHIP:
+        return
+    h, k = topo.host(core), core % 8
+    S = T.sem
+    X = bass.RemoteDMATransfer
+
+    def dst(d):
+        rid, pid = topo.addr(d, core)
+        return bass.DstId(rid=rid, pnc=pid)
+
+    hl = [L for L in LANES if L[0] != RK]
+    own = [L for L in LANES if L[0] == RK]
+    sc_eng = 1
+    while hl and sc_eng * 2 * len(hl) <= 16:
+        sc_eng *= 2
+
+    if k != RK:
+        mine = [L for L in hl if L[0] == k]
+        if not mine:
+            return
+        c0, c1, d1 = mine[0][1], mine[0][2], mine[0][3]
+        d2 = other(d1)
+        g.wait_ge(S.own_arr, sc_eng)
+        rid, pid = topo.addr(at(nbr(h, d1), k), core)
+        g.remote_dma(T.R1[:, c0:c1], T.A[:, c0:c1], S.r1_0, S.sent, pid, rid, 0x00FF)
+        g.wait_ge(S.r1_0, 8)
+        g.remote_dma_fused([
+            X(dst_ids=[dst(at(nbr(h, d2), RK))], dma_engine_mask=0x00FF, remote_sem=S.r2_arr,
+              srcs=[T.A[:, c0:c1], T.R1[:, c0:c1]], dsts=[T.R2[:, c0:c1]], alu_op=1),
+            X(dst_ids=[dst(at(h, RK))], dma_engine_mask=0xFF00, remote_sem=S.p_arr,
+              srcs=[T.A[:, c0:c1], T.R1[:, c0:c1]], dsts=[T.P[:, c0:c1]], alu_op=1),
+        ], local_sem=S.sent)
+        g.wait_ge(S.sent, 24)
+        return
+
+    r = T.rank_of(core)
+    sent = 0
+    r1sem = [S.r1_0, S.r1_1]
+    if hl:
+        hc0, hc1 = min(L[1] for L in hl), max(L[2] for L in hl)
+        g.dma_start(T.A[:, hc0:hc1], T.x2[:, hc0:hc1]).then_inc(S.ld_h, 16)
+    if own:
+        oc0, oc1 = min(L[1] for L in own), max(L[2] for L in own)
+        g.dma_start(T.A[:, oc0:oc1], T.x2[:, oc0:oc1]).then_inc(S.ld_o, 16)
+    g.dma_start(T.X1[:], T.x1[:]).then_inc(S.ld_x, 16)
+
+    if hl:
+        g.wait_ge(S.ld_h, 16)
+        tr = []
+        for i, L in enumerate(hl):
+            m = ((1 << sc_eng) - 1) << (i * sc_eng)
+            tr.append(X(dst_ids=[dst(at(h, L[0]))], dma_engine_mask=m, remote_sem=S.own_arr,
+                        src=T.A[:, L[1]:L[2]], dst=T.A[:, L[1]:L[2]]))
+        g.remote_dma_fused(tr, local_sem=S.sent)
+        sent += sc_eng * len(hl)
+    oe = 8 // len(own) if own else 0
+    if own:
+        g.wait_ge(S.ld_o, 16)
+        tr = []
+        for i, L in enumerate(own):
+            m = ((1 << oe) - 1) << (i * oe)
+            tr.append(X(dst_ids=[dst(at(nbr(h, L[3]), RK))], dma_engine_mask=m, remote_sem=r1sem[i],
+                        src=T.A[:, L[1]:L[2]], dst=T.R1[:, L[1]:L[2]]))
+        g.remote_dma_fused(tr, local_sem=S.sent)
+        sent += 8
+
+    a, b, d = r ^ 1, 3 - r, r ^ 2
+    g.wait_ge(S.ld_x, 16)
+    g.remote_dma_fused([
+        X(dst_ids=[dst(T.cores[a])], dma_engine_mask=0x03, remote_sem=S.y1_arr, src=T.X1[:, a:a + 1], dst=T.Y1B[:, r:r + 1]),
+        X(dst_ids=[dst(T.cores[b])], dma_engine_mask=0x0C, remote_sem=S.y1_arr, src=T.X1[:, b:b + 1], dst=T.Y1B[:, r:r + 1]),
+        X(dst_ids=[dst(T.cores[a])], dma_engine_mask=0x30, remote_sem=S.fw_arr, src=T.X1[:, d:d + 1], dst=T.FW[:, 0:1]),
+    ], local_sem=S.sent)
+    sent += 6
+    g.dma_start(T.Y1B[:, r:r + 1], T.X1[:, r:r + 1]).then_inc(S.l_c, 16)
+    if own:
+        g.dma_start(T.y2[:, oc0:oc1], T.A[:, oc0:oc1]).then_inc(S.cp_o, 16)
+        for i, L in enumerate(own):
+            m = ((1 << oe) - 1) << (i * oe)
+            g.wait_ge(r1sem[i], oe)
+            g.remote_dma_fused([
+                X(dst_ids=[dst(at(nbr(h, other(L[3])), RK))], dma_engine_mask=m, remote_sem=S.r2_arr,
+                  srcs=[T.A[:, L[1]:L[2]], T.R1[:, L[1]:L[2]]], dsts=[T.R2[:, L[1]:L[2]]], alu_op=1)],
+                local_sem=S.sent)
+            sent += oe
+    g.wait_ge(S.fw_arr, 2)
+    rid, pid = topo.addr(T.cores[b], core)
+    g.remote_dma(T.Y1B[:, a:a + 1], T.FW[:, 0:1], S.y1_arr, S.sent, pid, rid, 0x00FF)
+    sent += 8
+    if own:
+        g.wait_ge(S.cp_o, 16)
+        g.dma_start(T.y2[:, oc0:oc1], T.R1[:, oc0:oc1], accum_op=AluOpType.add).then_inc(S.ac_o, 16)
+    if hl:
+        g.wait_ge(S.p_arr, 8 * len(hl))
+        g.dma_start(T.y2[:, hc0:hc1], T.P[:, hc0:hc1]).then_inc(S.cp_h, 16)
+    g.wait_ge(S.r2_arr, 8 * len(hl) + oe * len(own))
+    if own:
+        g.wait_ge(S.ac_o, 16)
+    if hl:
+        g.wait_ge(S.cp_h, 16)
+    g.dma_start(T.y2[:], T.R2[:], accum_op=AluOpType.add).then_inc(S.fin, 16)
+    g.wait_ge(S.y1_arr, 12)
+    g.wait_ge(S.l_c, 16)
+    g.dma_start(T.y1[:], T.Y1B[:]).then_inc(S.st1, 16)
+    g.wait_ge(S.sent, sent)
+    g.wait_ge(S.st1, 16)
+    g.wait_ge(S.fin, 16)

@@ -1,22 +1,22 @@
 import concourse.bass as bass
-from concourse.mybir import AluOpType
 
 W = 896
 CHIP, RK = 4, 6
-LANES = ((0, 0, 128, "A"), (1, 128, 256, "B"), (2, 256, 384, "A"), (3, 384, 512, "B"),
-         (4, 512, 640, "A"), (5, 640, 768, "B"), (7, 768, 896, "A"))
+WAVES = (((0, 0, 128, "A"), (1, 128, 256, "B"), (4, 256, 384, "A"), (5, 384, 512, "B")),
+         ((2, 512, 640, "A"), (3, 640, 768, "B"), (7, 768, 896, "A")))
+SC_ENG = 4
 
 SCRATCH = {
     "A": ("sbuf", [128, W], "float32"),
     "R1": ("sbuf", [128, W], "float32"),
-    "P": ("sbuf", [128, W], "float32"),
     "R2": ("sbuf", [128, W], "float32"),
+    "P": ("sbuf", [128, W], "float32"),
     "X1": ("sbuf", [128, 4], "float32"),
     "Y1B": ("sbuf", [128, 4], "float32"),
     "FW": ("sbuf", [128, 1], "float32"),
 }
-SEMAPHORES = ["ld_h", "ld_o", "ld_x", "l_c", "cp_o", "ac_o", "cp_h", "fin", "st1",
-              "own_arr", "r1_0", "r1_1", "p_arr", "r2_arr", "fw_arr", "y1_arr", "sent"]
+SEMAPHORES = ["ld_0", "ld_1", "ld_x", "l_c", "st_0", "st_1", "st1",
+              "own_arr", "r1_arr", "r2_arr", "p_0", "p_1", "fw_arr", "y1_arr", "sent"]
 
 
 def nbr(h, side):
@@ -37,66 +37,47 @@ def rank_program(g, core, T, topo):
     h, k = topo.host(core), core % 8
     S = T.sem
     X = bass.RemoteDMATransfer
+    psem = [S.p_0, S.p_1]
 
     def dst(d):
         rid, pid = topo.addr(d, core)
         return bass.DstId(rid=rid, pnc=pid)
 
-    hl = [L for L in LANES if L[0] != RK]
-    own = [L for L in LANES if L[0] == RK]
-    sc_eng = 1
-    while hl and sc_eng * 2 * len(hl) <= 16:
-        sc_eng *= 2
-
     if k != RK:
-        mine = [L for L in hl if L[0] == k]
-        if not mine:
-            return
-        c0, c1, d1 = mine[0][1], mine[0][2], mine[0][3]
-        d2 = other(d1)
-        g.wait_ge(S.own_arr, sc_eng)
-        rid, pid = topo.addr(at(nbr(h, d1), k), core)
-        g.remote_dma(T.R1[:, c0:c1], T.A[:, c0:c1], S.r1_0, S.sent, pid, rid, 0x00FF)
-        g.wait_ge(S.r1_0, 8)
-        g.remote_dma_fused([
-            X(dst_ids=[dst(at(nbr(h, d2), RK))], dma_engine_mask=0x00FF, remote_sem=S.r2_arr,
-              srcs=[T.A[:, c0:c1], T.R1[:, c0:c1]], dsts=[T.R2[:, c0:c1]], alu_op=1),
-            X(dst_ids=[dst(at(h, RK))], dma_engine_mask=0xFF00, remote_sem=S.p_arr,
-              srcs=[T.A[:, c0:c1], T.R1[:, c0:c1]], dsts=[T.P[:, c0:c1]], alu_op=1),
-        ], local_sem=S.sent)
-        g.wait_ge(S.sent, 24)
+        for w, lanes in enumerate(WAVES):
+            for L in lanes:
+                if L[0] != k:
+                    continue
+                c0, c1, d1 = L[1], L[2], L[3]
+                own, r1, r2 = T.A[:, c0:c1], T.R1[:, c0:c1], T.R2[:, c0:c1]
+                g.wait_ge(S.own_arr, SC_ENG)
+                rid, pid = topo.addr(at(nbr(h, d1), k), core)
+                g.remote_dma(r1, own, S.r1_arr, S.sent, pid, rid, 0x00FF)
+                g.wait_ge(S.r1_arr, 8)
+                g.remote_dma_fused([X(dst_ids=[dst(at(nbr(h, other(d1)), k))], dma_engine_mask=0x00FF, remote_sem=S.r2_arr,
+                                      srcs=[own, r1], dsts=[r2], alu_op=1)], local_sem=S.sent)
+                g.wait_ge(S.r2_arr, 8)
+                g.remote_dma_fused([X(dst_ids=[dst(at(h, RK))], dma_engine_mask=0xFFFF, remote_sem=psem[w],
+                                      srcs=[own, r1, r2], dsts=[T.P[:, c0:c1]], alu_op=1)], local_sem=S.sent)
+                g.wait_ge(S.sent, 32)
         return
 
     r = T.rank_of(core)
     sent = 0
-    r1sem = [S.r1_0, S.r1_1]
-    if hl:
-        hc0, hc1 = min(L[1] for L in hl), max(L[2] for L in hl)
-        g.dma_start(T.A[:, hc0:hc1], T.x2[:, hc0:hc1]).then_inc(S.ld_h, 16)
-    if own:
-        oc0, oc1 = min(L[1] for L in own), max(L[2] for L in own)
-        g.dma_start(T.A[:, oc0:oc1], T.x2[:, oc0:oc1]).then_inc(S.ld_o, 16)
+    ld, st = [S.ld_0, S.ld_1], [S.st_0, S.st_1]
+    span = [(min(L[1] for L in lanes), max(L[2] for L in lanes)) for lanes in WAVES]
+    for w, (c0, c1) in enumerate(span):
+        g.dma_start(T.A[:, c0:c1], T.x2[:, c0:c1]).then_inc(ld[w], 16)
     g.dma_start(T.X1[:], T.x1[:]).then_inc(S.ld_x, 16)
-
-    if hl:
-        g.wait_ge(S.ld_h, 16)
+    for w, lanes in enumerate(WAVES):
+        g.wait_ge(ld[w], 16)
         tr = []
-        for i, L in enumerate(hl):
-            m = ((1 << sc_eng) - 1) << (i * sc_eng)
+        for i, L in enumerate(lanes):
+            m = ((1 << SC_ENG) - 1) << (i * SC_ENG)
             tr.append(X(dst_ids=[dst(at(h, L[0]))], dma_engine_mask=m, remote_sem=S.own_arr,
                         src=T.A[:, L[1]:L[2]], dst=T.A[:, L[1]:L[2]]))
         g.remote_dma_fused(tr, local_sem=S.sent)
-        sent += sc_eng * len(hl)
-    oe = 8 // len(own) if own else 0
-    if own:
-        g.wait_ge(S.ld_o, 16)
-        tr = []
-        for i, L in enumerate(own):
-            m = ((1 << oe) - 1) << (i * oe)
-            tr.append(X(dst_ids=[dst(at(nbr(h, L[3]), RK))], dma_engine_mask=m, remote_sem=r1sem[i],
-                        src=T.A[:, L[1]:L[2]], dst=T.R1[:, L[1]:L[2]]))
-        g.remote_dma_fused(tr, local_sem=S.sent)
-        sent += 8
+        sent += SC_ENG * len(lanes)
 
     a, b, d = r ^ 1, 3 - r, r ^ 2
     g.wait_ge(S.ld_x, 16)
@@ -107,35 +88,17 @@ def rank_program(g, core, T, topo):
     ], local_sem=S.sent)
     sent += 6
     g.dma_start(T.Y1B[:, r:r + 1], T.X1[:, r:r + 1]).then_inc(S.l_c, 16)
-    if own:
-        g.dma_start(T.y2[:, oc0:oc1], T.A[:, oc0:oc1]).then_inc(S.cp_o, 16)
-        for i, L in enumerate(own):
-            m = ((1 << oe) - 1) << (i * oe)
-            g.wait_ge(r1sem[i], oe)
-            g.remote_dma_fused([
-                X(dst_ids=[dst(at(nbr(h, other(L[3])), RK))], dma_engine_mask=m, remote_sem=S.r2_arr,
-                  srcs=[T.A[:, L[1]:L[2]], T.R1[:, L[1]:L[2]]], dsts=[T.R2[:, L[1]:L[2]]], alu_op=1)],
-                local_sem=S.sent)
-            sent += oe
     g.wait_ge(S.fw_arr, 2)
     rid, pid = topo.addr(T.cores[b], core)
     g.remote_dma(T.Y1B[:, a:a + 1], T.FW[:, 0:1], S.y1_arr, S.sent, pid, rid, 0x00FF)
     sent += 8
-    if own:
-        g.wait_ge(S.cp_o, 16)
-        g.dma_start(T.y2[:, oc0:oc1], T.R1[:, oc0:oc1], accum_op=AluOpType.add).then_inc(S.ac_o, 16)
-    if hl:
-        g.wait_ge(S.p_arr, 8 * len(hl))
-        g.dma_start(T.y2[:, hc0:hc1], T.P[:, hc0:hc1]).then_inc(S.cp_h, 16)
-    g.wait_ge(S.r2_arr, 8 * len(hl) + oe * len(own))
-    if own:
-        g.wait_ge(S.ac_o, 16)
-    if hl:
-        g.wait_ge(S.cp_h, 16)
-    g.dma_start(T.y2[:], T.R2[:], accum_op=AluOpType.add).then_inc(S.fin, 16)
     g.wait_ge(S.y1_arr, 12)
     g.wait_ge(S.l_c, 16)
     g.dma_start(T.y1[:], T.Y1B[:]).then_inc(S.st1, 16)
+    for w, (c0, c1) in enumerate(span):
+        g.wait_ge(psem[w], 16 * len(WAVES[w]))
+        g.dma_start(T.y2[:, c0:c1], T.P[:, c0:c1]).then_inc(st[w], 16)
     g.wait_ge(S.sent, sent)
     g.wait_ge(S.st1, 16)
-    g.wait_ge(S.fin, 16)
+    for w in range(len(WAVES)):
+        g.wait_ge(st[w], 16)

@@ -2,8 +2,8 @@ import concourse.bass as bass
 
 W = 896
 CHIP, RK = 4, 6
-WAVES = (((0, 0, 128, "A"), (1, 128, 256, "B"), (4, 256, 384, "A"), (5, 384, 512, "B")),
-         ((2, 512, 640, "A"), (3, 640, 768, "B"), (7, 768, 896, "A")))
+WAVES = (((0, 0, 128, "B"), (2, 128, 256, "B"), (4, 256, 384, "B"), (7, 384, 512, "B")),
+         ((1, 512, 640, "B"), (3, 640, 768, "B"), (5, 768, 896, "B")))
 SC_ENG = 4
 
 SCRATCH = {
@@ -49,16 +49,24 @@ def rank_program(g, core, T, topo):
                 if L[0] != k:
                     continue
                 c0, c1, d1 = L[1], L[2], L[3]
-                own, r1, r2 = T.A[:, c0:c1], T.R1[:, c0:c1], T.R2[:, c0:c1]
+                mid = (c0 + c1) // 2
+                q = h // 2 if d1 == "B" else (0, 1, 1, 0)[h]
+                k0, k1 = (c0, mid) if q == 0 else (mid, c1)
+                g0, g1 = (mid, c1) if q == 0 else (c0, mid)
+                own, r1, r2 = T.A[:, k0:k1], T.R1[:, k0:k1], T.R2[:, k0:k1]
                 g.wait_ge(S.own_arr, SC_ENG)
                 rid, pid = topo.addr(at(nbr(h, d1), k), core)
-                g.remote_dma(r1, own, S.r1_arr, S.sent, pid, rid, 0x00FF)
+                g.remote_dma(T.R1[:, g0:g1], T.A[:, g0:g1], S.r1_arr, S.sent, pid, rid, 0x00FF)
                 g.wait_ge(S.r1_arr, 8)
                 g.remote_dma_fused([X(dst_ids=[dst(at(nbr(h, other(d1)), k))], dma_engine_mask=0x00FF, remote_sem=S.r2_arr,
                                       srcs=[own, r1], dsts=[r2], alu_op=1)], local_sem=S.sent)
                 g.wait_ge(S.r2_arr, 8)
-                g.remote_dma_fused([X(dst_ids=[dst(at(h, RK))], dma_engine_mask=0xFFFF, remote_sem=psem[w],
-                                      srcs=[own, r1, r2], dsts=[T.P[:, c0:c1]], alu_op=1)], local_sem=S.sent)
+                g.remote_dma_fused([
+                    X(dst_ids=[dst(at(nbr(h, d1), RK))], dma_engine_mask=0x00FF, remote_sem=psem[w],
+                      srcs=[own, r1, r2], dsts=[T.P[:, k0:k1]], alu_op=1),
+                    X(dst_ids=[dst(at(h, RK))], dma_engine_mask=0xFF00, remote_sem=psem[w],
+                      srcs=[own, r1, r2], dsts=[T.P[:, k0:k1]], alu_op=1),
+                ], local_sem=S.sent)
                 g.wait_ge(S.sent, 32)
         return
 

@@ -3,7 +3,7 @@ import concourse.bass as bass
 W = 896
 CHIP, RK = 4, 6
 WAVES = (((0, 0, 128, "B"), (2, 128, 256, "B"), (4, 256, 384, "B"), (7, 384, 512, "B")),
-         ((1, 512, 640, "B"), (3, 640, 768, "B"), (5, 768, 896, "B")))
+         ((1, 512, 640, "A"), (3, 640, 768, "A"), (5, 768, 896, "A")))
 SC_ENG = 4
 
 SCRATCH = {

@@ -2,9 +2,10 @@ import concourse.bass as bass
 
 W = 896
 CHIP, RK = 4, 6
-WAVES = (((0, 0, 128, "B"), (2, 128, 256, "B"), (4, 256, 384, "B"), (7, 384, 512, "B")),
+WAVES = (((0, 0, 128, "A"), (2, 128, 256, "A"), (4, 256, 384, "A"), (7, 384, 512, "A")),
          ((1, 512, 640, "A"), (3, 640, 768, "A"), (5, 768, 896, "A")))
-SC_ENG = 4
+DIRECT = (True, True)
+SC_ENG = (2, 2)
 
 SCRATCH = {
     "A": ("sbuf", [128, W], "float32"),
@@ -31,6 +32,13 @@ def at(h, k):
     return h * 128 + CHIP * 8 + k
 
 
+def halves(h, L):
+    c0, c1 = L[1], L[2]
+    mid = (c0 + c1) // 2
+    q = h // 2 if L[3] == "B" else (0, 1, 1, 0)[h]
+    return ((c0, mid), (mid, c1)) if q == 0 else ((mid, c1), (c0, mid))
+
+
 def rank_program(g, core, T, topo):
     if topo.chip(core) != CHIP:
         return
@@ -48,16 +56,18 @@ def rank_program(g, core, T, topo):
             for L in lanes:
                 if L[0] != k:
                     continue
-                c0, c1, d1 = L[1], L[2], L[3]
-                mid = (c0 + c1) // 2
-                q = h // 2 if d1 == "B" else (0, 1, 1, 0)[h]
-                k0, k1 = (c0, mid) if q == 0 else (mid, c1)
-                g0, g1 = (mid, c1) if q == 0 else (c0, mid)
+                d1 = L[3]
+                (k0, k1), (g0, g1) = halves(h, L)
                 own, r1, r2 = T.A[:, k0:k1], T.R1[:, k0:k1], T.R2[:, k0:k1]
-                g.wait_ge(S.own_arr, SC_ENG)
-                rid, pid = topo.addr(at(nbr(h, d1), k), core)
-                g.remote_dma(T.R1[:, g0:g1], T.A[:, g0:g1], S.r1_arr, S.sent, pid, rid, 0x00FF)
-                g.wait_ge(S.r1_arr, 8)
+                sent = 24
+                g.wait_ge(S.own_arr, SC_ENG[w])
+                if DIRECT[w]:
+                    g.wait_ge(S.r1_arr, SC_ENG[w])
+                else:
+                    rid, pid = topo.addr(at(nbr(h, d1), k), core)
+                    g.remote_dma(T.R1[:, g0:g1], T.A[:, g0:g1], S.r1_arr, S.sent, pid, rid, 0x00FF)
+                    sent += 8
+                    g.wait_ge(S.r1_arr, 8)
                 g.remote_dma_fused([X(dst_ids=[dst(at(nbr(h, other(d1)), k))], dma_engine_mask=0x00FF, remote_sem=S.r2_arr,
                                       srcs=[own, r1], dsts=[r2], alu_op=1)], local_sem=S.sent)
                 g.wait_ge(S.r2_arr, 8)
@@ -67,7 +77,7 @@ def rank_program(g, core, T, topo):
                     X(dst_ids=[dst(at(h, RK))], dma_engine_mask=0xFF00, remote_sem=psem[w],
                       srcs=[own, r1, r2], dsts=[T.P[:, k0:k1]], alu_op=1),
                 ], local_sem=S.sent)
-                g.wait_ge(S.sent, 32)
+                g.wait_ge(S.sent, sent)
         return
 
     r = T.rank_of(core)
@@ -79,13 +89,22 @@ def rank_program(g, core, T, topo):
     g.dma_start(T.X1[:], T.x1[:]).then_inc(S.ld_x, 16)
     for w, lanes in enumerate(WAVES):
         g.wait_ge(ld[w], 16)
+        e = SC_ENG[w]
         tr = []
         for i, L in enumerate(lanes):
-            m = ((1 << SC_ENG) - 1) << (i * SC_ENG)
-            tr.append(X(dst_ids=[dst(at(h, L[0]))], dma_engine_mask=m, remote_sem=S.own_arr,
-                        src=T.A[:, L[1]:L[2]], dst=T.A[:, L[1]:L[2]]))
+            m = ((1 << e) - 1) << (i * e)
+            if DIRECT[w]:
+                (k0, k1), (g0, g1) = halves(h, L)
+                tr.append(X(dst_ids=[dst(at(nbr(h, L[3]), L[0]))], dma_engine_mask=m, remote_sem=S.r1_arr,
+                            src=T.A[:, g0:g1], dst=T.R1[:, g0:g1]))
+                tr.append(X(dst_ids=[dst(at(h, L[0]))], dma_engine_mask=m << 8, remote_sem=S.own_arr,
+                            src=T.A[:, k0:k1], dst=T.A[:, k0:k1]))
+                sent += 2 * e
+            else:
+                tr.append(X(dst_ids=[dst(at(h, L[0]))], dma_engine_mask=m, remote_sem=S.own_arr,
+                            src=T.A[:, L[1]:L[2]], dst=T.A[:, L[1]:L[2]]))
+                sent += e
         g.remote_dma_fused(tr, local_sem=S.sent)
-        sent += SC_ENG * len(lanes)
 
     a, b, d = r ^ 1, 3 - r, r ^ 2
     g.wait_ge(S.ld_x, 16)

import concourse.bass as bass

W = 896
CHIP, RK = 4, 6
WAVES = (((0, 0, 128, "A"), (2, 128, 256, "A"), (4, 256, 384, "A"), (7, 384, 512, "A")),
         ((1, 512, 640, "A"), (3, 640, 768, "A"), (5, 768, 896, "A")))
DIRECT = (True, True)
SC_ENG = (2, 2)

SCRATCH = {
    "A": ("sbuf", [128, W], "float32"),
    "R1": ("sbuf", [128, W], "float32"),
    "R2": ("sbuf", [128, W], "float32"),
    "P": ("sbuf", [128, W], "float32"),
    "X1": ("sbuf", [128, 4], "float32"),
    "Y1B": ("sbuf", [128, 4], "float32"),
    "FW": ("sbuf", [128, 1], "float32"),
}
SEMAPHORES = ["ld_0", "ld_1", "ld_x", "l_c", "st_0", "st_1", "st1",
              "own_arr", "r1_arr", "r2_arr", "p_0", "p_1", "fw_arr", "y1_arr", "sent"]


def nbr(h, side):
    return h ^ 1 if side == "A" else 3 - h


def other(side):
    return "B" if side == "A" else "A"


def at(h, k):
    return h * 128 + CHIP * 8 + k


def halves(h, L):
    c0, c1 = L[1], L[2]
    mid = (c0 + c1) // 2
    q = h // 2 if L[3] == "B" else (0, 1, 1, 0)[h]
    return ((c0, mid), (mid, c1)) if q == 0 else ((mid, c1), (c0, mid))


def rank_program(g, core, T, topo):
    if topo.chip(core) != CHIP:
        return
    h, k = topo.host(core), core % 8
    S = T.sem
    X = bass.RemoteDMATransfer
    psem = [S.p_0, S.p_1]

    def dst(d):
        rid, pid = topo.addr(d, core)
        return bass.DstId(rid=rid, pnc=pid)

    if k != RK:
        for w, lanes in enumerate(WAVES):
            for L in lanes:
                if L[0] != k:
                    continue
                d1 = L[3]
                (k0, k1), (g0, g1) = halves(h, L)
                own, r1, r2 = T.A[:, k0:k1], T.R1[:, k0:k1], T.R2[:, k0:k1]
                sent = 24
                g.wait_ge(S.own_arr, SC_ENG[w])
                if DIRECT[w]:
                    g.wait_ge(S.r1_arr, SC_ENG[w])
                else:
                    rid, pid = topo.addr(at(nbr(h, d1), k), core)
                    g.remote_dma(T.R1[:, g0:g1], T.A[:, g0:g1], S.r1_arr, S.sent, pid, rid, 0x00FF)
                    sent += 8
                    g.wait_ge(S.r1_arr, 8)
                g.remote_dma_fused([X(dst_ids=[dst(at(nbr(h, other(d1)), k))], dma_engine_mask=0x00FF, remote_sem=S.r2_arr,
                                      srcs=[own, r1], dsts=[r2], alu_op=1)], local_sem=S.sent)
                g.wait_ge(S.r2_arr, 8)
                g.remote_dma_fused([
                    X(dst_ids=[dst(at(nbr(h, d1), RK))], dma_engine_mask=0x00FF, remote_sem=psem[w],
                      srcs=[own, r1, r2], dsts=[T.P[:, k0:k1]], alu_op=1),
                    X(dst_ids=[dst(at(h, RK))], dma_engine_mask=0xFF00, remote_sem=psem[w],
                      srcs=[own, r1, r2], dsts=[T.P[:, k0:k1]], alu_op=1),
                ], local_sem=S.sent)
                g.wait_ge(S.sent, sent)
        return

    r = T.rank_of(core)
    sent = 0
    ld, st = [S.ld_0, S.ld_1], [S.st_0, S.st_1]
    span = [(min(L[1] for L in lanes), max(L[2] for L in lanes)) for lanes in WAVES]
    for w, (c0, c1) in enumerate(span):
        g.dma_start(T.A[:, c0:c1], T.x2[:, c0:c1]).then_inc(ld[w], 16)
    g.dma_start(T.X1[:], T.x1[:]).then_inc(S.ld_x, 16)
    for w, lanes in enumerate(WAVES):
        g.wait_ge(ld[w], 16)
        e = SC_ENG[w]
        tr = []
        for i, L in enumerate(lanes):
            m = ((1 << e) - 1) << (i * e)
            if DIRECT[w]:
                (k0, k1), (g0, g1) = halves(h, L)
                tr.append(X(dst_ids=[dst(at(nbr(h, L[3]), L[0]))], dma_engine_mask=m, remote_sem=S.r1_arr,
                            src=T.A[:, g0:g1], dst=T.R1[:, g0:g1]))
                tr.append(X(dst_ids=[dst(at(h, L[0]))], dma_engine_mask=m << 8, remote_sem=S.own_arr,
                            src=T.A[:, k0:k1], dst=T.A[:, k0:k1]))
                sent += 2 * e
            else:
                tr.append(X(dst_ids=[dst(at(h, L[0]))], dma_engine_mask=m, remote_sem=S.own_arr,
                            src=T.A[:, L[1]:L[2]], dst=T.A[:, L[1]:L[2]]))
                sent += e
        g.remote_dma_fused(tr, local_sem=S.sent)

    a, b, d = r ^ 1, 3 - r, r ^ 2
    g.wait_ge(S.ld_x, 16)
    g.remote_dma_fused([
        X(dst_ids=[dst(T.cores[a])], dma_engine_mask=0x03, remote_sem=S.y1_arr, src=T.X1[:, a:a + 1], dst=T.Y1B[:, r:r + 1]),
        X(dst_ids=[dst(T.cores[b])], dma_engine_mask=0x0C, remote_sem=S.y1_arr, src=T.X1[:, b:b + 1], dst=T.Y1B[:, r:r + 1]),
        X(dst_ids=[dst(T.cores[a])], dma_engine_mask=0x30, remote_sem=S.fw_arr, src=T.X1[:, d:d + 1], dst=T.FW[:, 0:1]),
    ], local_sem=S.sent)
    sent += 6
    g.dma_start(T.Y1B[:, r:r + 1], T.X1[:, r:r + 1]).then_inc(S.l_c, 16)
    g.wait_ge(S.fw_arr, 2)
    rid, pid = topo.addr(T.cores[b], core)
    g.remote_dma(T.Y1B[:, a:a + 1], T.FW[:, 0:1], S.y1_arr, S.sent, pid, rid, 0x00FF)
    sent += 8
    g.wait_ge(S.y1_arr, 12)
    g.wait_ge(S.l_c, 16)
    g.dma_start(T.y1[:], T.Y1B[:]).then_inc(S.st1, 16)
    for w, (c0, c1) in enumerate(span):
        g.wait_ge(psem[w], 16 * len(WAVES[w]))
        g.dma_start(T.y2[:, c0:c1], T.P[:, c0:c1]).then_inc(st[w], 16)
    g.wait_ge(S.sent, sent)
    g.wait_ge(S.st1, 16)
    for w in range(len(WAVES)):
        g.wait_ge(st[w], 16)
